import numpy as np
import ml_dtypes


def mxq(x, axis, fmt="e4m3"):
    dtype, down = {"e4m3": (ml_dtypes.float8_e4m3fn, 7), "e5m2": (ml_dtypes.float8_e5m2, 14)}[fmt]
    v = np.moveaxis(np.asarray(x, np.float32).astype(ml_dtypes.bfloat16).astype(np.float64), axis, -1)
    blocks = v.reshape(v.shape[:-1] + (-1, 32))
    amax = np.abs(blocks).max(-1, keepdims=True)
    byte = np.maximum(np.where(amax > 0, np.frexp(amax)[1] - 1 + 127, 0) - down, 1)
    scale = np.exp2(byte - 127.0)
    codes = (blocks / scale).astype(np.float32).astype(dtype).astype(np.float64)
    return np.moveaxis((codes * scale).reshape(v.shape), -1, axis)


WIDE = False


def mx_kscale(k):
    if not WIDE:
        return np.ones(k)
    levels = np.array([10, -10, 5, -5, 0])
    if k % 512:
        return np.exp2(np.random.permutation(np.resize(levels, k // 32))).repeat(32)
    a = np.empty((k // 512, 16))
    for p in range(k // 512):
        a[p, :8] = np.random.permutation(np.resize(levels, 8))
        for g in range(8):
            far = levels[np.abs(levels - a[p, g]) >= 10]
            a[p, g + 8] = far[np.random.randint(len(far))]
    return np.exp2(a.ravel()).repeat(32)


def f64(x):
    return np.asarray(x).astype(np.float64)


def striped(idx):
    return np.tile(idx.reshape(-1, 16).T, (8, 1)).astype(np.uint16)


def unstriped(offs):
    return offs[:16].T.reshape(-1).astype(np.int64)


def striped8(idx):
    return np.concatenate([x.reshape(-1, 16).T for x in idx]).astype(np.uint16)


def runs(offs, k):
    lists = np.stack([offs[16 * r : 16 * r + 16].T.reshape(-1) for r in range(8)]).astype(np.int64)
    return lists[np.arange(k) % 512 // 64]


def pack_weight(w):
    k, n = w.shape
    w = f64(np.asarray(w, np.float32).astype(ml_dtypes.bfloat16)).reshape(k // 32, 32, n)
    amax = np.abs(w).max(1)
    byte = np.clip(np.where(amax > 0, np.frexp(amax)[1] - 1 + 127 - 7, 1), 1, 254)
    scaled = (w * np.exp2(127.0 - byte)[:, None, :]).reshape(k, n).astype(np.float32)
    words = np.ascontiguousarray(scaled.reshape(k // 512, 128, 4, n).transpose(0, 1, 3, 2)).astype(ml_dtypes.float8_e4m3fn).view(np.uint8)
    return words, np.ascontiguousarray(byte.astype(np.uint8).reshape(k // 512, 16, n))


def unpack_weight(words, scales):
    g, p, n, _ = words.shape
    vals = np.ascontiguousarray(words).view(ml_dtypes.float8_e4m3fn).astype(np.float64) * np.repeat(np.exp2(scales.astype(np.float64) - 127.0), 8, axis=1)[..., None]
    return vals.transpose(0, 1, 3, 2).reshape(g * 512, n)


def sigmoid(v):
    return 1.0 / (1.0 + np.exp(-np.maximum(v, -700.0)))

def planes(y):
    n, m = y.shape
    v = y.astype(np.float32).astype(ml_dtypes.bfloat16).astype(np.float64).reshape(n // 32, 32, m)
    top = np.abs(v).max(1)
    byte = np.clip(np.where(top > 0, np.frexp(top)[1] - 1 + 127 - 7, 1), 1, 254)
    codes = (v * np.exp2(127.0 - byte)[:, None, :]).reshape(n, m).astype(np.float32).astype(ml_dtypes.float8_e4m3fn).view(np.uint8)
    words = codes.reshape(n // 512, 128, 4, m).transpose(0, 1, 3, 2)
    return np.ascontiguousarray(words), np.ascontiguousarray(byte.astype(np.uint8).reshape(n // 512, 16, m))


K, T, S, N, H, W, G = 512, 2048, 512, 512, 512, 256, 2048


def setup_inputs():
    n = np.random.standard_normal
    s = mx_kscale(K)[:, None]
    u = mx_kscale(S)
    packed_xT = pack_weight(n((K, T)) * s)
    packed_w1 = pack_weight(n((K, H)) / np.sqrt(K) / s)
    packed_w2 = pack_weight(n((H, N)) / np.sqrt(H) / u[:, None])
    packed_dT = pack_weight(n((K, G)) / s)
    perm = np.stack([np.random.permutation(S) for _ in range(8)])
    return {
        "x_words": packed_xT[0],
        "x_scales": packed_xT[1],
        "w1_words": packed_w1[0],
        "w1_scales": packed_w1[1],
        "gn": (np.random.uniform(0.5, 1.5, (H, 1)) * u[:, None]).astype(np.float32),
        "w2_words": packed_w2[0],
        "w2_scales": packed_w2[1],
        "d_words": packed_dT[0],
        "d_scales": packed_dT[1],
        "offs": striped(np.random.permutation(T)[:S]),
        "n1": striped8(perm[:, :W]),
        "n2": striped8(perm[:, W:]),
        "two": striped(np.random.permutation(T)[:S]),
        "k1": striped8(np.random.randint(0, G, (8, H))),
        "n3": striped(np.random.permutation(S)),
        "n4": striped(np.random.permutation(S)),
    }


def reference(x_words, x_scales, w1_words, w1_scales, gn, w2_words, w2_scales, d_words, d_scales, offs, n1, n2, two, k1, n3, n4):
    xq = unpack_weight(x_words, x_scales)[:, unstriped(offs)]
    y = unpack_weight(w1_words, w1_scales).T @ xq
    pa = y[np.arange(H)[:, None], runs(n1, H)]
    pb = y[np.arange(H)[:, None], runs(n2, H)]
    ra = pa * sigmoid(pb)
    ds = y.copy()
    ds[np.arange(H)[:, None], runs(n2, H)] = ra
    z = f64(gn) * ds
    a = unpack_weight(w2_words, w2_scales).T @ mxq(z, 0, "e4m3")
    d_k1 = unpack_weight(d_words, d_scales)[np.arange(K)[:, None], runs(k1, K)]
    x_two = unpack_weight(x_words, x_scales)[:, unstriped(two)]
    b = 0.0625 * (d_k1.T @ x_two)
    out_0 = a + (sigmoid(b[:, unstriped(n4)] - b)) * (a[:, unstriped(n3)] - a)
    return (out_0,) + planes(out_0)

@@ -1,0 +1,240 @@
+from contextlib import ExitStack
+
+import concourse.mybir as mybir
+
+F32 = mybir.dt.float32
+BF16 = mybir.dt.bfloat16
+I32 = mybir.dt.int32
+U32 = mybir.dt.uint32
+U16 = mybir.dt.uint16
+U8 = mybir.dt.uint8
+FP8X4 = mybir.dt.float8_e4m3fn_x4
+ACT = mybir.ActivationFunctionType
+ALU = mybir.AluOpType
+
+P = 128
+PACK = 4
+T = 2048
+S = 512
+W = 256
+HALF = 256
+CUTS = (0, 128, 256, 384, 512)
+FLOPS = 3 * 2 * 512 * 512 * 512
+
+
+def tile_picked_cdjoinpullbfold_none_po_kernel(
+    tc, x_words, x_scales, w1_words, w1_scales, gn, w2_words, w2_scales, d_words, d_scales,
+    offs, n1, n2, two, k1, n3, n4, out_0, out_1, out_2,
+):
+    nc = tc.nc
+    with ExitStack() as ctx:
+        pool = ctx.enter_context(tc.tile_pool(name="keep", bufs=1))
+        psum = ctx.enter_context(tc.psum_pool(name="psum", bufs=1))
+
+        def load_list(src, name):
+            tile = pool.tile([P, src.shape[1]], U16, name=name)
+            nc.sync.dma_start(tile[:], src)
+            return tile
+
+        def load_words(src, name):
+            tile = pool.tile([P, src.shape[2]], I32, name=name, align_bytes=64)
+            nc.sync.dma_start(tile[:], src[0].rearrange("p n t -> p (n t)").bitcast(I32))
+            return tile
+
+        def zeroed_bytes(width, name, engine):
+            tile = pool.tile([P, width], U8, name=name, align_bytes=64)
+            engine.memset(tile[:].bitcast(I32), 0)
+            return tile
+
+        def load_scales(queue, tile, src):
+            for q in range(4):
+                queue.dma_start(tile[32 * q : 32 * q + 4, :].bitcast(I32), src[0, 4 * q : 4 * q + 4, :].bitcast(I32))
+
+        def gather(window, offsets, dtype, name):
+            tile = pool.tile([P, S], dtype, name=name, align_bytes=64)
+            nc.vector.tensor_copy(tile[:], window.indirect(offsets[:]))
+            return tile
+
+        def deal_words(copy, src, name):
+            tile = pool.tile([P, S], U32, name=name, align_bytes=64)
+            copy(tile[:].rearrange("p (t m) -> p m t", t=PACK), src.rearrange("p (m t) -> p m t", t=PACK))
+            return tile
+
+        def deal_bytes(copy, src, name):
+            tile = pool.tile([P, S], U8, name=name, align_bytes=64)
+            copy(tile[:].rearrange("p (t m) -> p t m", t=PACK), src.rearrange("p (m t) -> p t m", t=PACK))
+            return tile
+
+        def product(bank, cols, lw, ls, t, rw, rs):
+            m = slice(t * P, (t + 1) * P)
+            nc.tensor.matmul_mx(
+                out=bank[:, cols], lhsT=lw[:, m].bitcast(FP8X4), lhsT_scale=ls[:, m],
+                rhs=rw[:, cols].bitcast(FP8X4), rhs_scale=rs[:, cols], start=True, stop=True,
+            )
+
+        xs = zeroed_bytes(T, "xs", nc.vector)
+        w1s = zeroed_bytes(S, "w1s", nc.vector)
+        dsc = zeroed_bytes(T, "dsc", nc.gpsimd)
+        w2s = zeroed_bytes(S, "w2s", nc.gpsimd)
+        dms = zeroed_bytes(S, "dms", nc.gpsimd)
+
+        w1w = load_words(w1_words, "w1w")
+        load_scales(nc.sync, xs, x_scales)
+        offs_t = load_list(offs, "offs_t")
+        two_t = load_list(two, "two_t")
+        xw = load_words(x_words, "xw")
+        load_scales(nc.sync, w1s, w1_scales)
+        for r in range(2):
+            nc.sync.dma_start(dsc[r:P:16, :].bitcast(I32), d_scales[0, r:16:2, :].bitcast(I32))
+        k1_t = load_list(k1, "k1_t")
+        dw = load_words(d_words, "dw")
+        n2_t = load_list(n2, "n2_t")
+        n1_t = load_list(n1, "n1_t")
+        gain = pool.tile([P, PACK], F32)
+        nc.sync.dma_start(gain[:], gn.rearrange("(p t) o -> p (t o)", t=PACK))
+
+        xq_s = gather(xs[:], offs_t, U8, "xq_s")
+        xt_s = gather(xs[:], two_t, U8, "xt_s")
+        w1w_d = deal_words(nc.scalar.copy, w1w[:].bitcast(U32), "w1w_d")
+        w1s_d = deal_bytes(nc.gpsimd.tensor_copy, w1s[:], "w1s_d")
+        xq_w = gather(xw[:].bitcast(U32), offs_t, U32, "xq_w")
+
+        whole = slice(0, S)
+        y_banks = [psum.tile([P, S], F32, name=f"y_bank{t}", tag=f"ya{t}") for t in range(PACK)]
+        ys = [pool.tile([P, S], F32, name=f"y{t}") for t in range(PACK)]
+        pa = [pool.tile([P, W], F32, name=f"pa{t}") for t in range(PACK)]
+        sb = [pool.tile([P, W], F32, name=f"sb{t}") for t in range(PACK)]
+        for t in range(PACK):
+            product(y_banks[t], whole, w1w_d, w1s_d, t, xq_w, xq_s)
+        for t in range(PACK):
+            nc.scalar.copy(ys[t][:], y_banks[t][:])
+            nc.scalar.activation(sb[t][:], ys[t][:].indirect(n2_t[:]), ACT.Sigmoid)
+            nc.scalar.activation(pa[t][:], ys[t][:].indirect(n1_t[:]), ACT.Copy)
+
+        xt_w = gather(xw[:].bitcast(U32), two_t, U32, "xt_w")
+        dq_s = gather(dsc[:], k1_t, U8, "dq_s")
+        dd_s = deal_bytes(nc.vector.tensor_copy, dq_s[:], "dd_s")
+        for i in range(4):
+            first = 16 * (i // 2) + i % 2
+            nc.sync.dma_start(dms[i:P:32, :].bitcast(I32), dd_s[first:P:32, :].bitcast(I32))
+
+        w2w = load_words(w2_words, "w2w")
+        load_scales(nc.sync, w2s, w2_scales)
+        w2s_d = deal_bytes(nc.gpsimd.tensor_copy, w2s[:], "w2s_d")
+        n4_t = load_list(n4, "n4_t")
+        n3_t = load_list(n3, "n3_t")
+        zb = pool.tile([P, PACK, S], BF16)
+
+        def scatter(t):
+            nc.vector.tensor_tensor(ys[t][:].indirect(n2_t[:]), pa[t][:], sb[t][:], ALU.mult)
+
+        def gained(t):
+            nc.vector.tensor_scalar(zb[:, t, :], ys[t][:], gain[:, t : t + 1], None, ALU.mult)
+
+        dq_w = gather(dw[:].bitcast(U32), k1_t, U32, "dq_w")
+        dd_w = deal_words(nc.vector.tensor_copy, dq_w[:], "dd_w")
+        scatter(0)
+        b_banks = [psum.tile([P, S], F32, name=f"b_bank{t}") for t in range(PACK)]
+        for t in range(PACK):
+            product(b_banks[t], whole, dd_w, dms, t, xt_w, xt_s)
+        w2w_d = deal_words(nc.scalar.copy, w2w[:].bitcast(U32), "w2w_d")
+        for t in range(1, PACK):
+            scatter(t)
+            gained(t - 1)
+        gained(PACK - 1)
+
+        halves = [slice(h * HALF, (h + 1) * HALF) for h in range(2)]
+        chunks = [slice(c0, c1) for c0, c1 in zip(CUTS, CUTS[1:])]
+        widths = [c.stop - c.start for c in chunks]
+        entries = [slice(c.start // 16, c.stop // 16) for c in chunks]
+        n_chunks = len(chunks)
+
+        bs = [pool.tile([P, S], F32, name=f"b{t}") for t in range(PACK)]
+        gate = [pool.tile([P, PACK, widths[h]], F32, name=f"gate{h}") for h in range(n_chunks)]
+        for t in range(PACK):
+            nc.scalar.copy(bs[t][:], b_banks[t][:])
+        for h in range(n_chunks):
+            for t in range(PACK):
+                nc.scalar.activation(gate[h][:, t, :], bs[t][:].indirect(n4_t[:, entries[h]]), ACT.Copy)
+
+        z_in = [pool.tile([P, HALF, PACK], BF16, name=f"z_in{h}", align_bytes=64) for h in range(2)]
+        z_w = pool.tile([P, S], U32, align_bytes=64)
+        z_s = pool.tile([P, S], U8, align_bytes=64)
+        for h in range(2):
+            nc.vector.tensor_copy(
+                z_in[h][:].rearrange("p (c i) t -> p c t i", i=4),
+                zb[:, :, halves[h]].rearrange("p t (c i) -> p c t i", i=4),
+            )
+        for h in range(2):
+            nc.vector.quantize_mx(z_w[:, halves[h]].bitcast(FP8X4), z_s[:, halves[h]], z_in[h][:].rearrange("p c t -> p (c t)"))
+
+        a_banks = [psum.tile([P, S], F32, name=f"a_bank{t}", tag=f"ya{t}") for t in range(PACK)]
+        for t in range(PACK):
+            product(a_banks[t], whole, w2w_d, w2s_d, t, z_w, z_s)
+
+        a_sb = [pool.tile([P, S], F32, name=f"a{t}") for t in range(PACK)]
+        pulled = [pool.tile([P, PACK, widths[h]], F32, name=f"pulled{h}") for h in range(n_chunks)]
+        stay = [pool.tile([P, PACK, widths[h]], F32, name=f"stay{h}") for h in range(n_chunks)]
+        o_in = [pool.tile([P, widths[h], PACK], BF16, name=f"o_in{h}", align_bytes=64) for h in range(n_chunks)]
+        o_w = [pool.tile([P, widths[h]], I32, name=f"o_w{h}", align_bytes=64) for h in range(n_chunks)]
+        o_s = pool.tile([P, S], U8, align_bytes=64)
+        out_rows = out_0.rearrange("(p t) j -> p t j", t=PACK)
+        out_words = out_1[0].rearrange("p n t -> p (n t)").bitcast(I32)
+
+        def make_gate(h):
+            for t in range(PACK):
+                nc.vector.tensor_tensor(gate[h][:, t, :], gate[h][:, t, :], b_banks[t][:, chunks[h]], ALU.subtract)
+            nc.scalar.activation(gate[h][:], gate[h][:], ACT.Sigmoid, scale=0.0625)
+
+        make_gate(0)
+        for t in range(PACK):
+            if t >= 2:
+                nc.scalar.copy(a_sb[t][:], a_banks[t][:])
+            else:
+                nc.vector.tensor_copy(a_sb[t][:], a_banks[t][:])
+        def pull(h):
+            for t in range(PACK):
+                nc.scalar.activation(pulled[h][:, t, :], a_sb[t][:].indirect(n3_t[:, entries[h]]), ACT.Copy)
+
+        def keep(h):
+            for t in range(PACK):
+                nc.vector.scalar_tensor_tensor(
+                    stay[h][:, t, :], gate[h][:, t, :], 1.0, a_banks[t][:, chunks[h]], ALU.subtract, ALU.mult
+                )
+
+        def weigh(h):
+            nc.vector.tensor_tensor(pulled[h][:], pulled[h][:], gate[h][:], ALU.mult)
+
+        def join(h):
+            nc.vector.tensor_tensor(pulled[h][:], pulled[h][:], stay[h][:], ALU.subtract)
+            nc.sync.dma_start(out_rows[:, :, chunks[h]], pulled[h][:])
+
+        def weave(h):
+            nc.vector.tensor_copy(
+                o_in[h][:].rearrange("p (c i) t -> p c t i", i=4),
+                pulled[h][:].rearrange("p t (c i) -> p c t i", i=4),
+            )
+
+        def pack(h):
+            nc.vector.quantize_mx(o_w[h][:].bitcast(FP8X4), o_s[:, chunks[h]], o_in[h][:].rearrange("p c t -> p (c t)"))
+            nc.sync.dma_start(out_words[:, chunks[h]], o_w[h][:])
+
+        make_gate(1)
+        for step in range(n_chunks + 3):
+            if step < n_chunks:
+                pull(step)
+                if step + 2 < n_chunks:
+                    make_gate(step + 2)
+            if 0 <= step - 3 < n_chunks:
+                pack(step - 3)
+            if step < n_chunks:
+                keep(step)
+            if 0 <= step - 2 < n_chunks:
+                weave(step - 2)
+            if step < n_chunks:
+                weigh(step)
+            if 0 <= step - 1 < n_chunks:
+                join(step - 1)
+        for q in range(4):
+            queue = nc.scalar if q % 2 == 0 else nc.sync
+            queue.dma_start(out_2[0, 4 * q : 4 * q + 4, :].bitcast(I32), o_s[32 * q : 32 * q + 4, :].bitcast(I32))

@@ -14,11 +14,15 @@ ALU = mybir.AluOpType
 
 P = 128
 PACK = 4
-T = 2048
+SCALE_ROWS = 16
+TABLE = 2048
 S = 512
-W = 256
-HALF = 256
-CUTS = (0, 128, 256, 384, 512)
+HALF = S // 2
+B_FACTOR = 0.0625
+Z_CUT = 128
+OUT_CUT = 160
+JOIN_LAG = 3
+VECTOR_PULL = 2
 FLOPS = 3 * 2 * 512 * 512 * 512
 
 
@@ -46,9 +50,9 @@ def tile_picked_cdjoinpullbfold_none_po_kernel(
             engine.memset(tile[:].bitcast(I32), 0)
             return tile
 
-        def load_scales(queue, tile, src):
-            for q in range(4):
-                queue.dma_start(tile[32 * q : 32 * q + 4, :].bitcast(I32), src[0, 4 * q : 4 * q + 4, :].bitcast(I32))
+        def load_scales(tile, src):
+            for i in range(PACK):
+                nc.sync.dma_start(tile[i:P:32, :].bitcast(I32), src[0, i:SCALE_ROWS:PACK, :].bitcast(I32))
 
         def gather(window, offsets, dtype, name):
             tile = pool.tile([P, S], dtype, name=name, align_bytes=64)
@@ -60,181 +64,190 @@ def tile_picked_cdjoinpullbfold_none_po_kernel(
             copy(tile[:].rearrange("p (t m) -> p m t", t=PACK), src.rearrange("p (m t) -> p m t", t=PACK))
             return tile
 
-        def deal_bytes(copy, src, name):
-            tile = pool.tile([P, S], U8, name=name, align_bytes=64)
+        def deal_bytes(copy, src, name, tag):
+            tile = pool.tile([P, S], U8, name=name, tag=tag, align_bytes=64)
             copy(tile[:].rearrange("p (t m) -> p t m", t=PACK), src.rearrange("p (m t) -> p t m", t=PACK))
             return tile
 
-        def product(bank, cols, lw, ls, t, rw, rs):
+        def product(bank, t, dealt_words, dealt_scales, moving_words, moving_scales):
             m = slice(t * P, (t + 1) * P)
             nc.tensor.matmul_mx(
-                out=bank[:, cols], lhsT=lw[:, m].bitcast(FP8X4), lhsT_scale=ls[:, m],
-                rhs=rw[:, cols].bitcast(FP8X4), rhs_scale=rs[:, cols], start=True, stop=True,
+                out=bank[:], lhsT=dealt_words[:, m].bitcast(FP8X4), lhsT_scale=dealt_scales[:, m],
+                rhs=moving_words[:].bitcast(FP8X4), rhs_scale=moving_scales[:], start=True, stop=True,
             )
 
-        xs = zeroed_bytes(T, "xs", nc.vector)
-        w1s = zeroed_bytes(S, "w1s", nc.vector)
-        dsc = zeroed_bytes(T, "dsc", nc.gpsimd)
-        w2s = zeroed_bytes(S, "w2s", nc.gpsimd)
-        dms = zeroed_bytes(S, "dms", nc.gpsimd)
+        def weave(copy, dst, src):
+            copy(dst.rearrange("p (c i) t -> p c t i", i=4), src.rearrange("p t (c i) -> p c t i", i=4))
 
-        w1w = load_words(w1_words, "w1w")
-        load_scales(nc.sync, xs, x_scales)
+        x_s = zeroed_bytes(TABLE, "x_s", nc.gpsimd)
+        w1_s = zeroed_bytes(S, "w1_s", nc.vector)
+        d_s = zeroed_bytes(TABLE, "d_s", nc.vector)
+        w2_s = zeroed_bytes(S, "w2_s", nc.vector)
+        d_placed_s = zeroed_bytes(S, "d_placed_s", nc.vector)
+
         offs_t = load_list(offs, "offs_t")
         two_t = load_list(two, "two_t")
-        xw = load_words(x_words, "xw")
-        load_scales(nc.sync, w1s, w1_scales)
+        load_scales(x_s, x_scales)
+        x_w = load_words(x_words, "x_w")
+        load_scales(w1_s, w1_scales)
+        w1_w = load_words(w1_words, "w1_w")
         for r in range(2):
-            nc.sync.dma_start(dsc[r:P:16, :].bitcast(I32), d_scales[0, r:16:2, :].bitcast(I32))
+            nc.sync.dma_start(d_s[r:P:16, :].bitcast(I32), d_scales[0, r:SCALE_ROWS:2, :].bitcast(I32))
         k1_t = load_list(k1, "k1_t")
-        dw = load_words(d_words, "dw")
+        d_w = load_words(d_words, "d_w")
         n2_t = load_list(n2, "n2_t")
         n1_t = load_list(n1, "n1_t")
         gain = pool.tile([P, PACK], F32)
         nc.sync.dma_start(gain[:], gn.rearrange("(p t) o -> p (t o)", t=PACK))
+        n4_t = load_list(n4, "n4_t")
 
-        xq_s = gather(xs[:], offs_t, U8, "xq_s")
-        xt_s = gather(xs[:], two_t, U8, "xt_s")
-        w1w_d = deal_words(nc.scalar.copy, w1w[:].bitcast(U32), "w1w_d")
-        w1s_d = deal_bytes(nc.gpsimd.tensor_copy, w1s[:], "w1s_d")
-        xq_w = gather(xw[:].bitcast(U32), offs_t, U32, "xq_w")
+        xq_s = gather(x_s[:], offs_t, U8, "xq_s")
+        xtwo_s = gather(x_s[:], two_t, U8, "xtwo_s")
+        w1_dealt_w = deal_words(nc.scalar.copy, w1_w[:].bitcast(U32), "w1_dealt_w")
+        w1_dealt_s = deal_bytes(nc.gpsimd.tensor_copy, w1_s[:], "w1_dealt_s", "w1_dealt_s")
+        xq_w = gather(x_w[:].bitcast(U32), offs_t, U32, "xq_w")
 
-        whole = slice(0, S)
-        y_banks = [psum.tile([P, S], F32, name=f"y_bank{t}", tag=f"ya{t}") for t in range(PACK)]
+        y_banks = [psum.tile([P, S], F32, name=f"y_bank{t}", tag=f"y_then_a{t}") for t in range(PACK)]
         ys = [pool.tile([P, S], F32, name=f"y{t}") for t in range(PACK)]
-        pa = [pool.tile([P, W], F32, name=f"pa{t}") for t in range(PACK)]
-        sb = [pool.tile([P, W], F32, name=f"sb{t}") for t in range(PACK)]
+        ra = [pool.tile([P, HALF], F32, name=f"ra{t}") for t in range(PACK)]
+        sig_pb = [pool.tile([P, HALF], F32, name=f"sig_pb{t}", align_bytes=64) for t in range(PACK)]
         for t in range(PACK):
-            product(y_banks[t], whole, w1w_d, w1s_d, t, xq_w, xq_s)
+            product(y_banks[t], t, w1_dealt_w, w1_dealt_s, xq_w, xq_s)
         for t in range(PACK):
             nc.scalar.copy(ys[t][:], y_banks[t][:])
-            nc.scalar.activation(sb[t][:], ys[t][:].indirect(n2_t[:]), ACT.Sigmoid)
-            nc.scalar.activation(pa[t][:], ys[t][:].indirect(n1_t[:]), ACT.Copy)
+            nc.scalar.activation(sig_pb[t][:], ys[t][:].indirect(n2_t[:]), ACT.Sigmoid)
 
-        xt_w = gather(xw[:].bitcast(U32), two_t, U32, "xt_w")
-        dq_s = gather(dsc[:], k1_t, U8, "dq_s")
-        dd_s = deal_bytes(nc.vector.tensor_copy, dq_s[:], "dd_s")
-        for i in range(4):
+        xtwo_w = gather(x_w[:].bitcast(U32), two_t, U32, "xtwo_w")
+        dq_s = gather(d_s[:], k1_t, U8, "dq_s")
+        d_dealt_s = deal_bytes(nc.vector.tensor_copy, dq_s[:], "d_dealt_s", "d_dealt_s")
+        for i in range(PACK):
             first = 16 * (i // 2) + i % 2
-            nc.sync.dma_start(dms[i:P:32, :].bitcast(I32), dd_s[first:P:32, :].bitcast(I32))
+            nc.sync.dma_start(d_placed_s[i:P:32, :].bitcast(I32), d_dealt_s[first:P:32, :].bitcast(I32))
 
-        w2w = load_words(w2_words, "w2w")
-        load_scales(nc.sync, w2s, w2_scales)
-        w2s_d = deal_bytes(nc.gpsimd.tensor_copy, w2s[:], "w2s_d")
-        n4_t = load_list(n4, "n4_t")
+        load_scales(w2_s, w2_scales)
+        w2_w = load_words(w2_words, "w2_w")
         n3_t = load_list(n3, "n3_t")
-        zb = pool.tile([P, PACK, S], BF16)
 
-        def scatter(t):
-            nc.vector.tensor_tensor(ys[t][:].indirect(n2_t[:]), pa[t][:], sb[t][:], ALU.mult)
-
-        def gained(t):
-            nc.vector.tensor_scalar(zb[:, t, :], ys[t][:], gain[:, t : t + 1], None, ALU.mult)
-
-        dq_w = gather(dw[:].bitcast(U32), k1_t, U32, "dq_w")
-        dd_w = deal_words(nc.vector.tensor_copy, dq_w[:], "dd_w")
-        scatter(0)
+        dq_w = gather(d_w[:].bitcast(U32), k1_t, U32, "dq_w")
+        d_dealt_w = deal_words(nc.vector.tensor_copy, dq_w[:], "d_dealt_w")
         b_banks = [psum.tile([P, S], F32, name=f"b_bank{t}") for t in range(PACK)]
         for t in range(PACK):
-            product(b_banks[t], whole, dd_w, dms, t, xt_w, xt_s)
-        w2w_d = deal_words(nc.scalar.copy, w2w[:].bitcast(U32), "w2w_d")
-        for t in range(1, PACK):
-            scatter(t)
-            gained(t - 1)
-        gained(PACK - 1)
+            product(b_banks[t], t, d_dealt_w, d_placed_s, xtwo_w, xtwo_s)
+
+        for t in range(PACK):
+            nc.vector.tensor_copy(ra[t][:], ys[t][:].indirect(n1_t[:]))
+            nc.gpsimd.tensor_tensor(ra[t][:], ra[t][:], sig_pb[t][:], ALU.mult)
+        w2_dealt_s = deal_bytes(nc.gpsimd.tensor_copy, w2_s[:], "w2_dealt_s", f"sig_pb{PACK - 1}")
+        for t in range(PACK):
+            nc.vector.tensor_copy(ys[t][:].indirect(n2_t[:]), ra[t][:])
 
         halves = [slice(h * HALF, (h + 1) * HALF) for h in range(2)]
-        chunks = [slice(c0, c1) for c0, c1 in zip(CUTS, CUTS[1:])]
-        widths = [c.stop - c.start for c in chunks]
-        entries = [slice(c.start // 16, c.stop // 16) for c in chunks]
-        n_chunks = len(chunks)
+        entries = [slice(c.start // 16, c.stop // 16) for c in halves]
+        pairs = [slice(0, 2), slice(2, 4)]
 
-        bs = [pool.tile([P, S], F32, name=f"b{t}") for t in range(PACK)]
-        gate = [pool.tile([P, PACK, widths[h]], F32, name=f"gate{h}") for h in range(n_chunks)]
+        b_sb = pool.tile([P, PACK, S], F32)
+        gate_first = pool.tile([P, PACK, HALF], F32)
+        fetched_early = pool.tile([P, 2, HALF], F32)
+        z_rows = pool.tile([P, PACK, S], BF16, name="z_rows", tag="w2_s", align_bytes=64)
+
+        def fetch(dst, h, t):
+            nc.scalar.activation(dst, b_sb[:, t, :].indirect(n4_t[:, entries[h]]), ACT.Copy)
+
+        for t in range(2):
+            nc.gpsimd.tensor_scalar(z_rows[:, t, :], ys[t][:], gain[:, t : t + 1], 0.0, ALU.mult, ALU.add)
         for t in range(PACK):
-            nc.scalar.copy(bs[t][:], b_banks[t][:])
-        for h in range(n_chunks):
-            for t in range(PACK):
-                nc.scalar.activation(gate[h][:, t, :], bs[t][:].indirect(n4_t[:, entries[h]]), ACT.Copy)
+            nc.scalar.copy(b_sb[:, t, :], b_banks[t][:])
+        for pair in pairs:
+            for t in range(pair.start, pair.stop):
+                fetch(gate_first[:, t, :], 0, t)
+            nc.gpsimd.tensor_tensor(gate_first[:, pair, :], gate_first[:, pair, :], b_sb[:, pair, halves[0]], ALU.subtract)
+        for t in range(2):
+            fetch(fetched_early[:, t, :], 1, t)
+        nc.scalar.activation(z_rows[:, 2, :], ys[2][:], ACT.Copy, scale=gain[:, 2:3])
+        nc.vector.tensor_scalar(z_rows[:, 3, :], ys[3][:], gain[:, 3:4], None, ALU.mult)
+        w2_dealt_w = deal_words(nc.scalar.copy, w2_w[:].bitcast(U32), "w2_dealt_w")
+        nc.scalar.activation(gate_first[:], gate_first[:], ACT.Sigmoid, scale=B_FACTOR)
 
-        z_in = [pool.tile([P, HALF, PACK], BF16, name=f"z_in{h}", align_bytes=64) for h in range(2)]
+        z_woven = [pool.tile([P, HALF, PACK], BF16, name=f"z_woven{h}", align_bytes=64) for h in range(2)]
         z_w = pool.tile([P, S], U32, align_bytes=64)
         z_s = pool.tile([P, S], U8, align_bytes=64)
+        weave(nc.vector.tensor_copy, z_woven[0][:], z_rows[:, :, halves[0]])
+        weave(nc.vector.tensor_copy, z_woven[1][:, :Z_CUT, :], z_rows[:, :, HALF : HALF + Z_CUT])
+        weave(nc.scalar.copy, z_woven[1][:, Z_CUT:, :], z_rows[:, :, HALF + Z_CUT :])
         for h in range(2):
-            nc.vector.tensor_copy(
-                z_in[h][:].rearrange("p (c i) t -> p c t i", i=4),
-                zb[:, :, halves[h]].rearrange("p t (c i) -> p c t i", i=4),
+            nc.vector.quantize_mx(
+                z_w[:, halves[h]].bitcast(FP8X4), z_s[:, halves[h]], z_woven[h][:].rearrange("p c t -> p (c t)")
             )
-        for h in range(2):
-            nc.vector.quantize_mx(z_w[:, halves[h]].bitcast(FP8X4), z_s[:, halves[h]], z_in[h][:].rearrange("p c t -> p (c t)"))
 
-        a_banks = [psum.tile([P, S], F32, name=f"a_bank{t}", tag=f"ya{t}") for t in range(PACK)]
+        a_banks = [psum.tile([P, S], F32, name=f"a_bank{t}", tag=f"y_then_a{t}") for t in range(PACK)]
         for t in range(PACK):
-            product(a_banks[t], whole, w2w_d, w2s_d, t, z_w, z_s)
+            product(a_banks[t], t, w2_dealt_w, w2_dealt_s, z_w, z_s)
 
-        a_sb = [pool.tile([P, S], F32, name=f"a{t}") for t in range(PACK)]
-        pulled = [pool.tile([P, PACK, widths[h]], F32, name=f"pulled{h}") for h in range(n_chunks)]
-        stay = [pool.tile([P, PACK, widths[h]], F32, name=f"stay{h}") for h in range(n_chunks)]
-        o_in = [pool.tile([P, widths[h], PACK], BF16, name=f"o_in{h}", align_bytes=64) for h in range(n_chunks)]
-        o_w = [pool.tile([P, widths[h]], I32, name=f"o_w{h}", align_bytes=64) for h in range(n_chunks)]
-        o_s = pool.tile([P, S], U8, align_bytes=64)
+        gate_second = pool.tile([P, PACK, HALF], F32, name="gate_second", tag="z_woven1", align_bytes=64)
+        fetched_late = pool.tile([P, 2, HALF], F32, name="fetched_late", tag="z_woven0", align_bytes=64)
+        nc.gpsimd.tensor_tensor(gate_second[:, pairs[0], :], fetched_early[:], b_sb[:, pairs[0], halves[1]], ALU.subtract)
+        for t in range(pairs[1].start, pairs[1].stop):
+            nc.vector.tensor_copy(fetched_late[:, t - pairs[1].start, :], b_sb[:, t, :].indirect(n4_t[:, entries[1]]))
+        nc.gpsimd.tensor_tensor(gate_second[:, pairs[1], :], fetched_late[:], b_sb[:, pairs[1], halves[1]], ALU.subtract)
+        gate = [gate_first, gate_second]
+
+        def squash_second(pair):
+            nc.scalar.activation(gate_second[:, pair, :], gate_second[:, pair, :], ACT.Sigmoid, scale=B_FACTOR)
+
+        a_sb = pool.tile([P, PACK, S], F32)
+        res = [pool.tile([P, PACK, HALF], F32, name=f"res{h}") for h in range(2)]
+        res_woven = [pool.tile([P, HALF, PACK], BF16, name=f"res_woven{h}", align_bytes=64) for h in range(2)]
+        out_s = pool.tile([P, S], U8, align_bytes=64)
         out_rows = out_0.rearrange("(p t) j -> p t j", t=PACK)
         out_words = out_1[0].rearrange("p n t -> p (n t)").bitcast(I32)
+        steps = [(h, t) for h in range(2) for t in range(PACK)]
+        last = len(steps) - 1
 
-        def make_gate(h):
-            for t in range(PACK):
-                nc.vector.tensor_tensor(gate[h][:, t, :], gate[h][:, t, :], b_banks[t][:, chunks[h]], ALU.subtract)
-            nc.scalar.activation(gate[h][:], gate[h][:], ACT.Sigmoid, scale=0.0625)
-
-        make_gate(0)
-        for t in range(PACK):
-            if t >= 2:
-                nc.scalar.copy(a_sb[t][:], a_banks[t][:])
+        def pull(i):
+            h, t = steps[i]
+            window = a_sb[:, t, :].indirect(n3_t[:, entries[h]])
+            if i == VECTOR_PULL:
+                nc.vector.tensor_copy(res[h][:, t, :], window)
             else:
-                nc.vector.tensor_copy(a_sb[t][:], a_banks[t][:])
-        def pull(h):
-            for t in range(PACK):
-                nc.scalar.activation(pulled[h][:, t, :], a_sb[t][:].indirect(n3_t[:, entries[h]]), ACT.Copy)
+                nc.scalar.activation(res[h][:, t, :], window, ACT.Copy)
+            nc.vector.tensor_tensor(res[h][:, t, :], res[h][:, t, :], a_banks[t][:, halves[h]], ALU.subtract)
 
-        def keep(h):
-            for t in range(PACK):
-                nc.vector.scalar_tensor_tensor(
-                    stay[h][:, t, :], gate[h][:, t, :], 1.0, a_banks[t][:, chunks[h]], ALU.subtract, ALU.mult
-                )
+        def weigh(engine, i):
+            h, t = steps[i]
+            engine.tensor_tensor(res[h][:, t : t + 1, :], res[h][:, t : t + 1, :], gate[h][:, t : t + 1, :], ALU.mult)
 
-        def weigh(h):
-            nc.vector.tensor_tensor(pulled[h][:], pulled[h][:], gate[h][:], ALU.mult)
+        def join(i):
+            h, t = steps[i]
+            nc.vector.tensor_tensor(res[h][:, t, :], res[h][:, t, :], a_banks[t][:, halves[h]], ALU.add)
+            if t % 2 == 1:
+                nc.sync.dma_start(out_rows[:, pairs[t // 2], halves[h]], res[h][:, pairs[t // 2], :])
 
-        def join(h):
-            nc.vector.tensor_tensor(pulled[h][:], pulled[h][:], stay[h][:], ALU.subtract)
-            nc.sync.dma_start(out_rows[:, :, chunks[h]], pulled[h][:])
+        nc.scalar.copy(a_sb[:, 0, :], a_banks[0][:])
+        squash_second(pairs[0])
+        for t in range(1, PACK):
+            nc.vector.tensor_copy(a_sb[:, t, :], a_banks[t][:])
+        for i in range(len(steps) + JOIN_LAG):
+            if i <= last:
+                pull(i)
+            if i == 1:
+                squash_second(pairs[1])
+            if i < last:
+                weigh(nc.gpsimd, i)
+            if i == last + JOIN_LAG - 1:
+                weigh(nc.vector, last)
+            if i >= JOIN_LAG:
+                join(i - JOIN_LAG)
+            if i - JOIN_LAG == PACK - 1:
+                weave(nc.scalar.copy, res_woven[0][:], res[0][:])
 
-        def weave(h):
-            nc.vector.tensor_copy(
-                o_in[h][:].rearrange("p (c i) t -> p c t i", i=4),
-                pulled[h][:].rearrange("p t (c i) -> p c t i", i=4),
+        weave(nc.vector.tensor_copy, res_woven[1][:, :OUT_CUT, :], res[1][:, :, :OUT_CUT])
+        weave(nc.scalar.copy, res_woven[1][:, OUT_CUT:, :], res[1][:, :, OUT_CUT:])
+        for h in range(2):
+            codes = pool.tile([P, HALF], I32, name=f"out_w{h}", align_bytes=64)
+            nc.vector.quantize_mx(
+                codes[:].bitcast(FP8X4), out_s[:, halves[h]], res_woven[h][:].rearrange("p c t -> p (c t)")
             )
-
-        def pack(h):
-            nc.vector.quantize_mx(o_w[h][:].bitcast(FP8X4), o_s[:, chunks[h]], o_in[h][:].rearrange("p c t -> p (c t)"))
-            nc.sync.dma_start(out_words[:, chunks[h]], o_w[h][:])
-
-        make_gate(1)
-        for step in range(n_chunks + 3):
-            if step < n_chunks:
-                pull(step)
-                if step + 2 < n_chunks:
-                    make_gate(step + 2)
-            if 0 <= step - 3 < n_chunks:
-                pack(step - 3)
-            if step < n_chunks:
-                keep(step)
-            if 0 <= step - 2 < n_chunks:
-                weave(step - 2)
-            if step < n_chunks:
-                weigh(step)
-            if 0 <= step - 1 < n_chunks:
-                join(step - 1)
-        for q in range(4):
-            queue = nc.scalar if q % 2 == 0 else nc.sync
-            queue.dma_start(out_2[0, 4 * q : 4 * q + 4, :].bitcast(I32), o_s[32 * q : 32 * q + 4, :].bitcast(I32))
+            nc.sync.dma_start(out_words[:, halves[h]], codes[:])
+        for i in range(PACK):
+            queue = nc.scalar if i % 2 == 0 else nc.sync
+            queue.dma_start(out_2[0, i:SCALE_ROWS:PACK, :].bitcast(I32), out_s[i:P:32, :].bitcast(I32))

from contextlib import ExitStack

import concourse.mybir as mybir

F32 = mybir.dt.float32
BF16 = mybir.dt.bfloat16
I32 = mybir.dt.int32
U32 = mybir.dt.uint32
U16 = mybir.dt.uint16
U8 = mybir.dt.uint8
FP8X4 = mybir.dt.float8_e4m3fn_x4
ACT = mybir.ActivationFunctionType
ALU = mybir.AluOpType

P = 128
PACK = 4
SCALE_ROWS = 16
TABLE = 2048
S = 512
HALF = S // 2
B_FACTOR = 0.0625
Z_CUT = 128
OUT_CUT = 160
JOIN_LAG = 3
VECTOR_PULL = 2
FLOPS = 3 * 2 * 512 * 512 * 512


def tile_picked_cdjoinpullbfold_none_po_kernel(
    tc, x_words, x_scales, w1_words, w1_scales, gn, w2_words, w2_scales, d_words, d_scales,
    offs, n1, n2, two, k1, n3, n4, out_0, out_1, out_2,
):
    nc = tc.nc
    with ExitStack() as ctx:
        pool = ctx.enter_context(tc.tile_pool(name="keep", bufs=1))
        psum = ctx.enter_context(tc.psum_pool(name="psum", bufs=1))

        def load_list(src, name):
            tile = pool.tile([P, src.shape[1]], U16, name=name)
            nc.sync.dma_start(tile[:], src)
            return tile

        def load_words(src, name):
            tile = pool.tile([P, src.shape[2]], I32, name=name, align_bytes=64)
            nc.sync.dma_start(tile[:], src[0].rearrange("p n t -> p (n t)").bitcast(I32))
            return tile

        def zeroed_bytes(width, name, engine):
            tile = pool.tile([P, width], U8, name=name, align_bytes=64)
            engine.memset(tile[:].bitcast(I32), 0)
            return tile

        def load_scales(tile, src):
            for i in range(PACK):
                nc.sync.dma_start(tile[i:P:32, :].bitcast(I32), src[0, i:SCALE_ROWS:PACK, :].bitcast(I32))

        def gather(window, offsets, dtype, name):
            tile = pool.tile([P, S], dtype, name=name, align_bytes=64)
            nc.vector.tensor_copy(tile[:], window.indirect(offsets[:]))
            return tile

        def deal_words(copy, src, name):
            tile = pool.tile([P, S], U32, name=name, align_bytes=64)
            copy(tile[:].rearrange("p (t m) -> p m t", t=PACK), src.rearrange("p (m t) -> p m t", t=PACK))
            return tile

        def deal_bytes(copy, src, name, tag):
            tile = pool.tile([P, S], U8, name=name, tag=tag, align_bytes=64)
            copy(tile[:].rearrange("p (t m) -> p t m", t=PACK), src.rearrange("p (m t) -> p t m", t=PACK))
            return tile

        def product(bank, t, dealt_words, dealt_scales, moving_words, moving_scales):
            m = slice(t * P, (t + 1) * P)
            nc.tensor.matmul_mx(
                out=bank[:], lhsT=dealt_words[:, m].bitcast(FP8X4), lhsT_scale=dealt_scales[:, m],
                rhs=moving_words[:].bitcast(FP8X4), rhs_scale=moving_scales[:], start=True, stop=True,
            )

        def weave(copy, dst, src):
            copy(dst.rearrange("p (c i) t -> p c t i", i=4), src.rearrange("p t (c i) -> p c t i", i=4))

        x_s = zeroed_bytes(TABLE, "x_s", nc.gpsimd)
        w1_s = zeroed_bytes(S, "w1_s", nc.vector)
        d_s = zeroed_bytes(TABLE, "d_s", nc.vector)
        w2_s = zeroed_bytes(S, "w2_s", nc.vector)
        d_placed_s = zeroed_bytes(S, "d_placed_s", nc.vector)

        offs_t = load_list(offs, "offs_t")
        two_t = load_list(two, "two_t")
        load_scales(x_s, x_scales)
        x_w = load_words(x_words, "x_w")
        load_scales(w1_s, w1_scales)
        w1_w = load_words(w1_words, "w1_w")
        for r in range(2):
            nc.sync.dma_start(d_s[r:P:16, :].bitcast(I32), d_scales[0, r:SCALE_ROWS:2, :].bitcast(I32))
        k1_t = load_list(k1, "k1_t")
        d_w = load_words(d_words, "d_w")
        n2_t = load_list(n2, "n2_t")
        n1_t = load_list(n1, "n1_t")
        gain = pool.tile([P, PACK], F32)
        nc.sync.dma_start(gain[:], gn.rearrange("(p t) o -> p (t o)", t=PACK))
        n4_t = load_list(n4, "n4_t")

        xq_s = gather(x_s[:], offs_t, U8, "xq_s")
        xtwo_s = gather(x_s[:], two_t, U8, "xtwo_s")
        w1_dealt_w = deal_words(nc.scalar.copy, w1_w[:].bitcast(U32), "w1_dealt_w")
        w1_dealt_s = deal_bytes(nc.gpsimd.tensor_copy, w1_s[:], "w1_dealt_s", "w1_dealt_s")
        xq_w = gather(x_w[:].bitcast(U32), offs_t, U32, "xq_w")

        y_banks = [psum.tile([P, S], F32, name=f"y_bank{t}", tag=f"y_then_a{t}") for t in range(PACK)]
        ys = [pool.tile([P, S], F32, name=f"y{t}") for t in range(PACK)]
        ra = [pool.tile([P, HALF], F32, name=f"ra{t}") for t in range(PACK)]
        sig_pb = [pool.tile([P, HALF], F32, name=f"sig_pb{t}", align_bytes=64) for t in range(PACK)]
        for t in range(PACK):
            product(y_banks[t], t, w1_dealt_w, w1_dealt_s, xq_w, xq_s)
        for t in range(PACK):
            nc.scalar.copy(ys[t][:], y_banks[t][:])
            nc.scalar.activation(sig_pb[t][:], ys[t][:].indirect(n2_t[:]), ACT.Sigmoid)

        xtwo_w = gather(x_w[:].bitcast(U32), two_t, U32, "xtwo_w")
        dq_s = gather(d_s[:], k1_t, U8, "dq_s")
        d_dealt_s = deal_bytes(nc.vector.tensor_copy, dq_s[:], "d_dealt_s", "d_dealt_s")
        for i in range(PACK):
            first = 16 * (i // 2) + i % 2
            nc.sync.dma_start(d_placed_s[i:P:32, :].bitcast(I32), d_dealt_s[first:P:32, :].bitcast(I32))

        load_scales(w2_s, w2_scales)
        w2_w = load_words(w2_words, "w2_w")
        n3_t = load_list(n3, "n3_t")

        dq_w = gather(d_w[:].bitcast(U32), k1_t, U32, "dq_w")
        d_dealt_w = deal_words(nc.vector.tensor_copy, dq_w[:], "d_dealt_w")
        b_banks = [psum.tile([P, S], F32, name=f"b_bank{t}") for t in range(PACK)]
        for t in range(PACK):
            product(b_banks[t], t, d_dealt_w, d_placed_s, xtwo_w, xtwo_s)

        for t in range(PACK):
            nc.vector.tensor_copy(ra[t][:], ys[t][:].indirect(n1_t[:]))
            nc.gpsimd.tensor_tensor(ra[t][:], ra[t][:], sig_pb[t][:], ALU.mult)
        w2_dealt_s = deal_bytes(nc.gpsimd.tensor_copy, w2_s[:], "w2_dealt_s", f"sig_pb{PACK - 1}")
        for t in range(PACK):
            nc.vector.tensor_copy(ys[t][:].indirect(n2_t[:]), ra[t][:])

        halves = [slice(h * HALF, (h + 1) * HALF) for h in range(2)]
        entries = [slice(c.start // 16, c.stop // 16) for c in halves]
        pairs = [slice(0, 2), slice(2, 4)]

        b_sb = pool.tile([P, PACK, S], F32)
        gate_first = pool.tile([P, PACK, HALF], F32)
        fetched_early = pool.tile([P, 2, HALF], F32)
        z_rows = pool.tile([P, PACK, S], BF16, name="z_rows", tag="w2_s", align_bytes=64)

        def fetch(dst, h, t):
            nc.scalar.activation(dst, b_sb[:, t, :].indirect(n4_t[:, entries[h]]), ACT.Copy)

        for t in range(2):
            nc.gpsimd.tensor_scalar(z_rows[:, t, :], ys[t][:], gain[:, t : t + 1], 0.0, ALU.mult, ALU.add)
        for t in range(PACK):
            nc.scalar.copy(b_sb[:, t, :], b_banks[t][:])
        for pair in pairs:
            for t in range(pair.start, pair.stop):
                fetch(gate_first[:, t, :], 0, t)
            nc.gpsimd.tensor_tensor(gate_first[:, pair, :], gate_first[:, pair, :], b_sb[:, pair, halves[0]], ALU.subtract)
        for t in range(2):
            fetch(fetched_early[:, t, :], 1, t)
        nc.scalar.activation(z_rows[:, 2, :], ys[2][:], ACT.Copy, scale=gain[:, 2:3])
        nc.vector.tensor_scalar(z_rows[:, 3, :], ys[3][:], gain[:, 3:4], None, ALU.mult)
        w2_dealt_w = deal_words(nc.scalar.copy, w2_w[:].bitcast(U32), "w2_dealt_w")
        nc.scalar.activation(gate_first[:], gate_first[:], ACT.Sigmoid, scale=B_FACTOR)

        z_woven = [pool.tile([P, HALF, PACK], BF16, name=f"z_woven{h}", align_bytes=64) for h in range(2)]
        z_w = pool.tile([P, S], U32, align_bytes=64)
        z_s = pool.tile([P, S], U8, align_bytes=64)
        weave(nc.vector.tensor_copy, z_woven[0][:], z_rows[:, :, halves[0]])
        weave(nc.vector.tensor_copy, z_woven[1][:, :Z_CUT, :], z_rows[:, :, HALF : HALF + Z_CUT])
        weave(nc.scalar.copy, z_woven[1][:, Z_CUT:, :], z_rows[:, :, HALF + Z_CUT :])
        for h in range(2):
            nc.vector.quantize_mx(
                z_w[:, halves[h]].bitcast(FP8X4), z_s[:, halves[h]], z_woven[h][:].rearrange("p c t -> p (c t)")
            )

        a_banks = [psum.tile([P, S], F32, name=f"a_bank{t}", tag=f"y_then_a{t}") for t in range(PACK)]
        for t in range(PACK):
            product(a_banks[t], t, w2_dealt_w, w2_dealt_s, z_w, z_s)

        gate_second = pool.tile([P, PACK, HALF], F32, name="gate_second", tag="z_woven1", align_bytes=64)
        fetched_late = pool.tile([P, 2, HALF], F32, name="fetched_late", tag="z_woven0", align_bytes=64)
        nc.gpsimd.tensor_tensor(gate_second[:, pairs[0], :], fetched_early[:], b_sb[:, pairs[0], halves[1]], ALU.subtract)
        for t in range(pairs[1].start, pairs[1].stop):
            nc.vector.tensor_copy(fetched_late[:, t - pairs[1].start, :], b_sb[:, t, :].indirect(n4_t[:, entries[1]]))
        nc.gpsimd.tensor_tensor(gate_second[:, pairs[1], :], fetched_late[:], b_sb[:, pairs[1], halves[1]], ALU.subtract)
        gate = [gate_first, gate_second]

        def squash_second(pair):
            nc.scalar.activation(gate_second[:, pair, :], gate_second[:, pair, :], ACT.Sigmoid, scale=B_FACTOR)

        a_sb = pool.tile([P, PACK, S], F32)
        res = [pool.tile([P, PACK, HALF], F32, name=f"res{h}") for h in range(2)]
        res_woven = [pool.tile([P, HALF, PACK], BF16, name=f"res_woven{h}", align_bytes=64) for h in range(2)]
        out_s = pool.tile([P, S], U8, align_bytes=64)
        out_rows = out_0.rearrange("(p t) j -> p t j", t=PACK)
        out_words = out_1[0].rearrange("p n t -> p (n t)").bitcast(I32)
        steps = [(h, t) for h in range(2) for t in range(PACK)]
        last = len(steps) - 1

        def pull(i):
            h, t = steps[i]
            window = a_sb[:, t, :].indirect(n3_t[:, entries[h]])
            if i == VECTOR_PULL:
                nc.vector.tensor_copy(res[h][:, t, :], window)
            else:
                nc.scalar.activation(res[h][:, t, :], window, ACT.Copy)
            nc.vector.tensor_tensor(res[h][:, t, :], res[h][:, t, :], a_banks[t][:, halves[h]], ALU.subtract)

        def weigh(engine, i):
            h, t = steps[i]
            engine.tensor_tensor(res[h][:, t : t + 1, :], res[h][:, t : t + 1, :], gate[h][:, t : t + 1, :], ALU.mult)

        def join(i):
            h, t = steps[i]
            nc.vector.tensor_tensor(res[h][:, t, :], res[h][:, t, :], a_banks[t][:, halves[h]], ALU.add)
            if t % 2 == 1:
                nc.sync.dma_start(out_rows[:, pairs[t // 2], halves[h]], res[h][:, pairs[t // 2], :])

        nc.scalar.copy(a_sb[:, 0, :], a_banks[0][:])
        squash_second(pairs[0])
        for t in range(1, PACK):
            nc.vector.tensor_copy(a_sb[:, t, :], a_banks[t][:])
        for i in range(len(steps) + JOIN_LAG):
            if i <= last:
                pull(i)
            if i == 1:
                squash_second(pairs[1])
            if i < last:
                weigh(nc.gpsimd, i)
            if i == last + JOIN_LAG - 1:
                weigh(nc.vector, last)
            if i >= JOIN_LAG:
                join(i - JOIN_LAG)
            if i - JOIN_LAG == PACK - 1:
                weave(nc.scalar.copy, res_woven[0][:], res[0][:])

        weave(nc.vector.tensor_copy, res_woven[1][:, :OUT_CUT, :], res[1][:, :, :OUT_CUT])
        weave(nc.scalar.copy, res_woven[1][:, OUT_CUT:, :], res[1][:, :, OUT_CUT:])
        for h in range(2):
            codes = pool.tile([P, HALF], I32, name=f"out_w{h}", align_bytes=64)
            nc.vector.quantize_mx(
                codes[:].bitcast(FP8X4), out_s[:, halves[h]], res_woven[h][:].rearrange("p c t -> p (c t)")
            )
            nc.sync.dma_start(out_words[:, halves[h]], codes[:])
        for i in range(PACK):
            queue = nc.scalar if i % 2 == 0 else nc.sync
            queue.dma_start(out_2[0, i:SCALE_ROWS:PACK, :].bitcast(I32), out_s[i:P:32, :].bitcast(I32))
